import numpy as np
import ml_dtypes


def mxq(x, axis, fmt="e4m3"):
    dtype, down = {"e4m3": (ml_dtypes.float8_e4m3fn, 7), "e5m2": (ml_dtypes.float8_e5m2, 14)}[fmt]
    v = np.moveaxis(np.asarray(x, np.float32).astype(ml_dtypes.bfloat16).astype(np.float64), axis, -1)
    blocks = v.reshape(v.shape[:-1] + (-1, 32))
    amax = np.abs(blocks).max(-1, keepdims=True)
    byte = np.maximum(np.where(amax > 0, np.frexp(amax)[1] - 1 + 127, 0) - down, 1)
    scale = np.exp2(byte - 127.0)
    codes = (blocks / scale).astype(np.float32).astype(dtype).astype(np.float64)
    return np.moveaxis((codes * scale).reshape(v.shape), -1, axis)


WIDE = False


def mx_kscale(k):
    if not WIDE:
        return np.ones(k)
    levels = np.array([10, -10, 5, -5, 0])
    if k % 512:
        return np.exp2(np.random.permutation(np.resize(levels, k // 32))).repeat(32)
    a = np.empty((k // 512, 16))
    for p in range(k // 512):
        a[p, :8] = np.random.permutation(np.resize(levels, 8))
        for g in range(8):
            far = levels[np.abs(levels - a[p, g]) >= 10]
            a[p, g + 8] = far[np.random.randint(len(far))]
    return np.exp2(a.ravel()).repeat(32)


def f64(x):
    return np.asarray(x).astype(np.float64)


def striped(idx):
    return np.tile(idx.reshape(-1, 16).T, (8, 1)).astype(np.uint16)


def unstriped(offs):
    return offs[:16].T.reshape(-1).astype(np.int64)


def pack_weight(w):
    k, n = w.shape
    w = f64(np.asarray(w, np.float32).astype(ml_dtypes.bfloat16)).reshape(k // 32, 32, n)
    amax = np.abs(w).max(1)
    byte = np.clip(np.where(amax > 0, np.frexp(amax)[1] - 1 + 127 - 7, 1), 1, 254)
    scaled = (w * np.exp2(127.0 - byte)[:, None, :]).reshape(k, n).astype(np.float32)
    words = np.ascontiguousarray(scaled.reshape(k // 512, 128, 4, n).transpose(0, 1, 3, 2)).astype(ml_dtypes.float8_e4m3fn).view(np.uint8)
    return words, np.ascontiguousarray(byte.astype(np.uint8).reshape(k // 512, 16, n))


def unpack_weight(words, scales):
    g, p, n, _ = words.shape
    vals = np.ascontiguousarray(words).view(ml_dtypes.float8_e4m3fn).astype(np.float64) * np.repeat(np.exp2(scales.astype(np.float64) - 127.0), 8, axis=1)[..., None]
    return vals.transpose(0, 1, 3, 2).reshape(g * 512, n)


def silu(v):
    return v / (1.0 + np.exp(-np.maximum(v, -700.0)))


K, T, E, C, N = 1024, 512, 8, 128, 128


def by_expert(wq, xq):
    return np.concatenate([wq[e].T @ xq[:, e * C:(e + 1) * C] for e in range(E)], axis=1)


def setup_inputs():
    n = np.random.standard_normal
    s = mx_kscale(K)[:, None]
    first = np.random.permutation(np.repeat(np.arange(E), T // E))
    second = (first + 1 + np.random.permutation(np.repeat(np.arange(E - 1), -(-T // (E - 1)))[:T])) % E
    while np.bincount(second, minlength=E).max() != T // E:
        load = np.bincount(second, minlength=E); hi, lo = int(load.argmax()), int(load.argmin())
        t = np.flatnonzero((second == hi) & (first != lo))[0]; second[t] = lo
    slot_token = np.empty(E * C, np.int64); pos = np.empty((2, T), np.int64); fill = np.zeros(E, np.int64)
    place = np.stack([np.random.permutation(C) for _ in range(E)])
    for r, deal in enumerate((first, second)):
        for t in np.random.permutation(T):
            e = deal[t]; j = e * C + place[e, fill[e]]; fill[e] += 1; slot_token[j] = t; pos[r, t] = j
    g = np.random.uniform(0.2, 0.8, T)
    packed = [pack_weight(m) for m in n((E, K, N)) / np.sqrt(K) / s[None]]
    return {
        "xT": (n((K, T)) * s).astype(np.float32),
        "w_words": np.stack([m[0] for m in packed]),
        "w_scales": np.stack([m[1] for m in packed]),
        "b": (0.3 * n((N, E))).astype(np.float32),
        "gate": np.stack([np.tile(g, (N, 1)), np.tile(1.0 - g, (N, 1))]).astype(np.float32),
        "offs": striped(slot_token),
        "pos1": striped(pos[0]),
        "pos2": striped(pos[1]),
    }


def reference(xT, w_words, w_scales, b, gate, offs, pos1, pos2):
    idx = unstriped(offs)
    xq = mxq(f64(xT)[:, idx], 0, "e4m3")
    w = np.stack([unpack_weight(w_words[e], w_scales[e]) for e in range(E)])
    y = by_expert(w, xq)
    y = silu(y + np.repeat(f64(b), C, axis=1))
    return f64(gate[0]) * y[:, unstriped(pos1)] + f64(gate[1]) * y[:, unstriped(pos2)]

@@ -1,0 +1,160 @@
+from contextlib import ExitStack
+
+import concourse.mybir as mybir
+
+K, T, E, C, N = 1024, 512, 8, 128, 128
+FLOPS = 2 * K * N * E * C
+
+F32 = mybir.dt.float32
+BF16 = mybir.dt.bfloat16
+I32 = mybir.dt.int32
+U32 = mybir.dt.uint32
+U16 = mybir.dt.uint16
+U8 = mybir.dt.uint8
+FP8X4 = mybir.dt.float8_e4m3fn_x4
+
+P = 128
+PACK = 4
+PASSES = K // (P * PACK)
+SLOTS = E * C
+SCALE_ROWS = 4
+
+X_CHUNKS = ((256, 256), (256, 256))
+VECTOR_SHARE = (160, 160)
+GATHER_PLAN = ((1024,), (512, 384, 128))
+WINDOW = (1536, 768)
+SCALE_WINDOW = 768
+PLANE = (0, 4)
+VECTOR_SHARE_1 = (0, 96)
+OUT_CHUNKS = (256, 256)
+
+
+def spans(widths):
+    edges = [sum(widths[:i]) for i in range(len(widths) + 1)]
+    return list(zip(edges[:-1], edges[1:]))
+
+
+def tile_routed_moe_kernel(tc, xT, w_words, w_scales, b, gate, offs, pos1, pos2, out):
+    nc = tc.nc
+    silu = mybir.ActivationFunctionType.Silu
+    mult, add = mybir.AluOpType.mult, mybir.AluOpType.add
+
+    with ExitStack() as ctx:
+        lists = ctx.enter_context(tc.tile_pool(name="lists", bufs=1))
+        keep = ctx.enter_context(tc.tile_pool(name="keep", bufs=1))
+        psum = ctx.enter_context(tc.psum_pool(name="psum", bufs=1))
+
+        offs_sb = lists.tile([P, SLOTS // 16], U16, name="offs_sb")
+        pos1_sb = lists.tile([P, T // 16], U16, name="pos1_sb")
+        pos2_sb = lists.tile([P, T // 16], U16, name="pos2_sb")
+
+        raw = [keep.tile([P, PACK, T], F32, name="raw%d" % a) for a in range(PASSES)]
+        xb = [keep.tile([P, T, PACK], BF16, name="xb%d" % a, align_bytes=64) for a in range(PASSES)]
+        xw = [keep.tile([P, WINDOW[a]], I32, name="xw%d" % a, align_bytes=64) for a in range(PASSES)]
+        xs = keep.tile([P, SCALE_WINDOW], U8, name="xs", align_bytes=64)
+        gw = keep.tile([P, PASSES, SLOTS], U32, name="gw", align_bytes=64)
+        gs = keep.tile([P, SLOTS], U8, name="gs", align_bytes=64)
+        ww = keep.tile([P, E * PASSES, N], I32, name="ww", align_bytes=64)
+        wsc = keep.tile([P, E * PASSES, N], U8, name="wsc", align_bytes=64)
+        b_sb = keep.tile([P, E], F32, name="b_sb")
+        gate_sb = keep.tile([P, 2, T], F32, name="gate_sb")
+        y = keep.tile([P, SLOTS], F32, name="y")
+        o1 = keep.tile([P, T], F32, name="o1")
+        o2 = keep.tile([P, T], F32, name="o2")
+        res = keep.tile([P, T], F32, name="res")
+        warm = keep.tile([P, 2], F32, name="warm")
+
+        nc.vector.memset(warm[:], 0.0)
+        nc.scalar.activation(out=warm[:, 1:2], in_=warm[:, 0:1], func=silu)
+        nc.vector.memset(xs[:].bitcast(I32), 0)
+        for a in range(PASSES):
+            nc.vector.memset(xw[a][:, T:WINDOW[a]], 0)
+        nc.vector.memset(wsc[:].rearrange("p a n -> p (a n)").bitcast(I32), 0)
+
+        x_view = xT.rearrange("(a p j) t -> a p j t", a=PASSES, p=P, j=PACK)
+        x_loads = [(a, t0, t1) for a in range(PASSES) for t0, t1 in spans(X_CHUNKS[a])]
+
+        def load_x(a, t0, t1):
+            nc.sync.dma_start(raw[a][:, :, t0:t1], x_view[a, :, :, t0:t1])
+
+        load_x(*x_loads[0])
+        nc.sync.dma_start(offs_sb[:], offs)
+        for x_load in x_loads[1:]:
+            load_x(*x_load)
+        nc.sync.dma_start(pos1_sb[:], pos1)
+        nc.sync.dma_start(pos2_sb[:], pos2)
+        s_view = w_scales.rearrange("e a (q r) n -> r q (e a) n", r=SCALE_ROWS)
+        for r in range(SCALE_ROWS):
+            nc.sync.dma_start(wsc[r:P:32, :, :].bitcast(I32), s_view[r].bitcast(I32))
+        w_view = w_words.rearrange("e a p n r -> p (e a) (n r)").bitcast(I32)
+        for i in range(0, E * PASSES, 4):
+            nc.sync.dma_start(ww[:, i:i + 4, :], w_view[:, i:i + 4, :])
+        nc.sync.dma_start(b_sb[:], b)
+        nc.sync.dma_start(gate_sb[:], gate.rearrange("g n t -> n g t"))
+
+        def interleave(engine_copy, a, t0, t1):
+            engine_copy(
+                out=xb[a][:, t0:t1, :].rearrange("p (c i) j -> p c j i", i=4),
+                in_=raw[a][:, :, t0:t1].rearrange("p j (c i) -> p c j i", i=4),
+            )
+
+        def interleave_shared(i):
+            t0, t1 = spans(X_CHUNKS[0])[i]
+            interleave(nc.vector.tensor_copy, 0, t0, t0 + VECTOR_SHARE[i])
+            interleave(nc.scalar.copy, 0, t0 + VECTOR_SHARE[i], t1)
+
+        def quantise(a, t0, t1):
+            nc.vector.quantize_mx(
+                out=xw[a][:, t0:t1].bitcast(FP8X4),
+                scales=xs[PLANE[a]:P, t0:t1],
+                in_=xb[a][:, t0:t1, :].rearrange("p t j -> p (t j)"),
+            )
+
+        interleave_shared(0)
+        quantise(0, 0, 256)
+        interleave_shared(1)
+        quantise(0, 256, 512)
+        for i, (t0, t1) in enumerate(spans(X_CHUNKS[1])):
+            interleave(nc.scalar.copy, 1, t0, t1 - VECTOR_SHARE_1[i])
+
+        acc = [psum.tile([P, C], F32, name="acc%d" % e) for e in range(E)]
+
+        def gather_words(a, s0, s1):
+            nc.vector.tensor_copy(gw[:, a, s0:s1], xw[a][:].bitcast(U32).indirect(offs_sb[:, s0 // 16:s1 // 16]))
+
+        def gather_scales(s0, s1):
+            nc.vector.tensor_copy(gs[:, s0:s1], xs[:].indirect(offs_sb[:, s0 // 16:s1 // 16]))
+
+        def multiply(a, e):
+            nc.tensor.matmul_mx(
+                out=acc[e][:],
+                lhsT=ww[:, e * PASSES + a, :].bitcast(FP8X4),
+                lhsT_scale=wsc[:, e * PASSES + a, :],
+                rhs=gw[:, a, e * C:(e + 1) * C].bitcast(FP8X4),
+                rhs_scale=gs[PLANE[a]:P, e * C:(e + 1) * C],
+                start=(a == 0),
+                stop=(a == PASSES - 1),
+            )
+
+        for s0, s1 in spans(GATHER_PLAN[0]):
+            gather_words(0, s0, s1)
+        for i, (t0, t1) in enumerate(spans(X_CHUNKS[1])):
+            if VECTOR_SHARE_1[i] > 0:
+                interleave(nc.vector.tensor_copy, 1, t1 - VECTOR_SHARE_1[i], t1)
+        for t0, t1 in spans(X_CHUNKS[1]):
+            quantise(1, t0, t1)
+        for s0, s1 in spans(GATHER_PLAN[1]):
+            gather_scales(s0, s1)
+            for e in range(s0 // C, s1 // C):
+                multiply(0, e)
+            gather_words(1, s0, s1)
+            for e in range(s0 // C, s1 // C):
+                multiply(1, e)
+                nc.scalar.activation(out=y[:, e * C:(e + 1) * C], in_=acc[e][:], func=silu, bias=b_sb[:, e:e + 1], scale=1.0)
+
+        nc.vector.tensor_tensor(out=o1[:], in0=y[:].indirect(pos1_sb[:]), in1=gate_sb[:, 0, :], op=mult)
+        for t0, t1 in spans(OUT_CHUNKS):
+            nc.vector.tensor_tensor(out=o2[:, t0:t1], in0=y[:].indirect(pos2_sb[:, t0 // 16:t1 // 16]), in1=gate_sb[:, 1, t0:t1], op=mult)
+        for t0, t1 in spans(OUT_CHUNKS):
+            nc.vector.tensor_tensor(out=res[:, t0:t1], in0=o1[:, t0:t1], in1=o2[:, t0:t1], op=add)
+            nc.sync.dma_start(out[:, t0:t1], res[:, t0:t1])

@@ -78,8 +78,9 @@ def tile_routed_moe_kernel(tc, xT, w_words, w_scales, b, gate, offs, pos1, pos2,
             nc.sync.dma_start(raw[a][:, :, t0:t1], x_view[a, :, :, t0:t1])
 
         load_x(*x_loads[0])
+        load_x(*x_loads[1])
         nc.sync.dma_start(offs_sb[:], offs)
-        for x_load in x_loads[1:]:
+        for x_load in x_loads[2:]:
             load_x(*x_load)
         nc.sync.dma_start(pos1_sb[:], pos1)
         nc.sync.dma_start(pos2_sb[:], pos2)
@@ -112,8 +113,11 @@ def tile_routed_moe_kernel(tc, xT, w_words, w_scales, b, gate, offs, pos1, pos2,
 
         interleave_shared(0)
         quantise(0, 0, 256)
-        interleave_shared(1)
-        quantise(0, 256, 512)
+        interleave(nc.scalar.copy, 0, 256 + VECTOR_SHARE[1], 512)
+        interleave(nc.vector.tensor_copy, 0, 256, 384)
+        interleave(nc.vector.tensor_copy, 0, 384, 256 + VECTOR_SHARE[1])
+        quantise(0, 256, 384)
+        quantise(0, 384, 512)
         for i, (t0, t1) in enumerate(spans(X_CHUNKS[1])):
             interleave(nc.scalar.copy, 1, t0, t1 - VECTOR_SHARE_1[i])
 

@@ -142,11 +142,10 @@ def tile_routed_moe_kernel(tc, xT, w_words, w_scales, b, gate, offs, pos1, pos2,
 
         for s0, s1 in spans(GATHER_PLAN[0]):
             gather_words(0, s0, s1)
-        for i, (t0, t1) in enumerate(spans(X_CHUNKS[1])):
-            if VECTOR_SHARE_1[i] > 0:
-                interleave(nc.vector.tensor_copy, 1, t1 - VECTOR_SHARE_1[i], t1)
-        for t0, t1 in spans(X_CHUNKS[1]):
-            quantise(1, t0, t1)
+        quantise(1, 0, 256)
+        interleave(nc.vector.tensor_copy, 1, T - VECTOR_SHARE_1[1], T)
+        quantise(1, 256, 384)
+        quantise(1, 384, 512)
         for s0, s1 in spans(GATHER_PLAN[1]):
             gather_scales(s0, s1)
             for e in range(s0 // C, s1 // C):

@@ -25,7 +25,6 @@ GATHER_PLAN = ((1024,), (512, 384, 128))
 WINDOW = (1536, 768)
 SCALE_WINDOW = 768
 PLANE = (0, 4)
-VECTOR_SHARE_1 = (0, 96)
 OUT_CHUNKS = (256, 256)
 
 
@@ -118,8 +117,8 @@ def tile_routed_moe_kernel(tc, xT, w_words, w_scales, b, gate, offs, pos1, pos2,
         interleave(nc.vector.tensor_copy, 0, 384, 256 + VECTOR_SHARE[1])
         quantise(0, 256, 384)
         quantise(0, 384, 512)
-        for i, (t0, t1) in enumerate(spans(X_CHUNKS[1])):
-            interleave(nc.scalar.copy, 1, t0, t1 - VECTOR_SHARE_1[i])
+        for t0, t1 in ((0, 256), (256, 384), (384, 512)):
+            interleave(nc.scalar.copy, 1, t0, t1)
 
         acc = [psum.tile([P, C], F32, name="acc%d" % e) for e in range(E)]
 
@@ -143,7 +142,6 @@ def tile_routed_moe_kernel(tc, xT, w_words, w_scales, b, gate, offs, pos1, pos2,
         for s0, s1 in spans(GATHER_PLAN[0]):
             gather_words(0, s0, s1)
         quantise(1, 0, 256)
-        interleave(nc.vector.tensor_copy, 1, T - VECTOR_SHARE_1[1], T)
         quantise(1, 256, 384)
         quantise(1, 384, 512)
         for s0, s1 in spans(GATHER_PLAN[1]):

@@ -19,7 +19,7 @@ PASSES = K // (P * PACK)
 SLOTS = E * C
 SCALE_ROWS = 4
 
-X_CHUNKS = ((256, 256), (256, 256))
+X_CHUNKS = ((256, 256), (192, 192, 128))
 VECTOR_SHARE = (160, 160)
 GATHER_PLAN = ((1024,), (512, 384, 128))
 WINDOW = (1536, 768)
@@ -117,7 +117,7 @@ def tile_routed_moe_kernel(tc, xT, w_words, w_scales, b, gate, offs, pos1, pos2,
         interleave(nc.vector.tensor_copy, 0, 384, 256 + VECTOR_SHARE[1])
         quantise(0, 256, 384)
         quantise(0, 384, 512)
-        for t0, t1 in ((0, 256), (256, 384), (384, 512)):
+        for t0, t1 in spans(X_CHUNKS[1]):
             interleave(nc.scalar.copy, 1, t0, t1)
 
         acc = [psum.tile([P, C], F32, name="acc%d" % e) for e in range(E)]
@@ -141,8 +141,8 @@ def tile_routed_moe_kernel(tc, xT, w_words, w_scales, b, gate, offs, pos1, pos2,
 
         for s0, s1 in spans(GATHER_PLAN[0]):
             gather_words(0, s0, s1)
-        quantise(1, 0, 256)
-        quantise(1, 256, 384)
+        quantise(1, 0, 128)
+        quantise(1, 128, 384)
         quantise(1, 384, 512)
         for s0, s1 in spans(GATHER_PLAN[1]):
             gather_scales(s0, s1)

@@ -94,8 +94,8 @@ def tile_routed_moe_kernel(tc, xT, w_words, w_scales, b, gate, offs, pos1, pos2,
 
         def interleave(engine_copy, a, t0, t1):
             engine_copy(
-                out=xb[a][:, t0:t1, :].rearrange("p (c i) j -> p c j i", i=4),
-                in_=raw[a][:, :, t0:t1].rearrange("p j (c i) -> p c j i", i=4),
+                out=xb[a][:, t0:t1, :].rearrange("p (c i) j -> p c j i", i=8),
+                in_=raw[a][:, :, t0:t1].rearrange("p j (c i) -> p c j i", i=8),
             )
 
         def interleave_shared(i):

from contextlib import ExitStack

import concourse.mybir as mybir

K, T, E, C, N = 1024, 512, 8, 128, 128
FLOPS = 2 * K * N * E * C

F32 = mybir.dt.float32
BF16 = mybir.dt.bfloat16
I32 = mybir.dt.int32
U32 = mybir.dt.uint32
U16 = mybir.dt.uint16
U8 = mybir.dt.uint8
FP8X4 = mybir.dt.float8_e4m3fn_x4

P = 128
PACK = 4
PASSES = K // (P * PACK)
SLOTS = E * C
SCALE_ROWS = 4

X_CHUNKS = ((256, 256), (192, 192, 128))
VECTOR_SHARE = (160, 160)
GATHER_PLAN = ((1024,), (512, 384, 128))
WINDOW = (1536, 768)
SCALE_WINDOW = 768
PLANE = (0, 4)
OUT_CHUNKS = (256, 256)


def spans(widths):
    edges = [sum(widths[:i]) for i in range(len(widths) + 1)]
    return list(zip(edges[:-1], edges[1:]))


def tile_routed_moe_kernel(tc, xT, w_words, w_scales, b, gate, offs, pos1, pos2, out):
    nc = tc.nc
    silu = mybir.ActivationFunctionType.Silu
    mult, add = mybir.AluOpType.mult, mybir.AluOpType.add

    with ExitStack() as ctx:
        lists = ctx.enter_context(tc.tile_pool(name="lists", bufs=1))
        keep = ctx.enter_context(tc.tile_pool(name="keep", bufs=1))
        psum = ctx.enter_context(tc.psum_pool(name="psum", bufs=1))

        offs_sb = lists.tile([P, SLOTS // 16], U16, name="offs_sb")
        pos1_sb = lists.tile([P, T // 16], U16, name="pos1_sb")
        pos2_sb = lists.tile([P, T // 16], U16, name="pos2_sb")

        raw = [keep.tile([P, PACK, T], F32, name="raw%d" % a) for a in range(PASSES)]
        xb = [keep.tile([P, T, PACK], BF16, name="xb%d" % a, align_bytes=64) for a in range(PASSES)]
        xw = [keep.tile([P, WINDOW[a]], I32, name="xw%d" % a, align_bytes=64) for a in range(PASSES)]
        xs = keep.tile([P, SCALE_WINDOW], U8, name="xs", align_bytes=64)
        gw = keep.tile([P, PASSES, SLOTS], U32, name="gw", align_bytes=64)
        gs = keep.tile([P, SLOTS], U8, name="gs", align_bytes=64)
        ww = keep.tile([P, E * PASSES, N], I32, name="ww", align_bytes=64)
        wsc = keep.tile([P, E * PASSES, N], U8, name="wsc", align_bytes=64)
        b_sb = keep.tile([P, E], F32, name="b_sb")
        gate_sb = keep.tile([P, 2, T], F32, name="gate_sb")
        y = keep.tile([P, SLOTS], F32, name="y")
        o1 = keep.tile([P, T], F32, name="o1")
        o2 = keep.tile([P, T], F32, name="o2")
        res = keep.tile([P, T], F32, name="res")
        warm = keep.tile([P, 2], F32, name="warm")

        nc.vector.memset(warm[:], 0.0)
        nc.scalar.activation(out=warm[:, 1:2], in_=warm[:, 0:1], func=silu)
        nc.vector.memset(xs[:].bitcast(I32), 0)
        for a in range(PASSES):
            nc.vector.memset(xw[a][:, T:WINDOW[a]], 0)
        nc.vector.memset(wsc[:].rearrange("p a n -> p (a n)").bitcast(I32), 0)

        x_view = xT.rearrange("(a p j) t -> a p j t", a=PASSES, p=P, j=PACK)
        x_loads = [(a, t0, t1) for a in range(PASSES) for t0, t1 in spans(X_CHUNKS[a])]

        def load_x(a, t0, t1):
            nc.sync.dma_start(raw[a][:, :, t0:t1], x_view[a, :, :, t0:t1])

        load_x(*x_loads[0])
        load_x(*x_loads[1])
        nc.sync.dma_start(offs_sb[:], offs)
        for x_load in x_loads[2:]:
            load_x(*x_load)
        nc.sync.dma_start(pos1_sb[:], pos1)
        nc.sync.dma_start(pos2_sb[:], pos2)
        s_view = w_scales.rearrange("e a (q r) n -> r q (e a) n", r=SCALE_ROWS)
        for r in range(SCALE_ROWS):
            nc.sync.dma_start(wsc[r:P:32, :, :].bitcast(I32), s_view[r].bitcast(I32))
        w_view = w_words.rearrange("e a p n r -> p (e a) (n r)").bitcast(I32)
        for i in range(0, E * PASSES, 4):
            nc.sync.dma_start(ww[:, i:i + 4, :], w_view[:, i:i + 4, :])
        nc.sync.dma_start(b_sb[:], b)
        nc.sync.dma_start(gate_sb[:], gate.rearrange("g n t -> n g t"))

        def interleave(engine_copy, a, t0, t1):
            engine_copy(
                out=xb[a][:, t0:t1, :].rearrange("p (c i) j -> p c j i", i=8),
                in_=raw[a][:, :, t0:t1].rearrange("p j (c i) -> p c j i", i=8),
            )

        def interleave_shared(i):
            t0, t1 = spans(X_CHUNKS[0])[i]
            interleave(nc.vector.tensor_copy, 0, t0, t0 + VECTOR_SHARE[i])
            interleave(nc.scalar.copy, 0, t0 + VECTOR_SHARE[i], t1)

        def quantise(a, t0, t1):
            nc.vector.quantize_mx(
                out=xw[a][:, t0:t1].bitcast(FP8X4),
                scales=xs[PLANE[a]:P, t0:t1],
                in_=xb[a][:, t0:t1, :].rearrange("p t j -> p (t j)"),
            )

        interleave_shared(0)
        quantise(0, 0, 256)
        interleave(nc.scalar.copy, 0, 256 + VECTOR_SHARE[1], 512)
        interleave(nc.vector.tensor_copy, 0, 256, 384)
        interleave(nc.vector.tensor_copy, 0, 384, 256 + VECTOR_SHARE[1])
        quantise(0, 256, 384)
        quantise(0, 384, 512)
        for t0, t1 in spans(X_CHUNKS[1]):
            interleave(nc.scalar.copy, 1, t0, t1)

        acc = [psum.tile([P, C], F32, name="acc%d" % e) for e in range(E)]

        def gather_words(a, s0, s1):
            nc.vector.tensor_copy(gw[:, a, s0:s1], xw[a][:].bitcast(U32).indirect(offs_sb[:, s0 // 16:s1 // 16]))

        def gather_scales(s0, s1):
            nc.vector.tensor_copy(gs[:, s0:s1], xs[:].indirect(offs_sb[:, s0 // 16:s1 // 16]))

        def multiply(a, e):
            nc.tensor.matmul_mx(
                out=acc[e][:],
                lhsT=ww[:, e * PASSES + a, :].bitcast(FP8X4),
                lhsT_scale=wsc[:, e * PASSES + a, :],
                rhs=gw[:, a, e * C:(e + 1) * C].bitcast(FP8X4),
                rhs_scale=gs[PLANE[a]:P, e * C:(e + 1) * C],
                start=(a == 0),
                stop=(a == PASSES - 1),
            )

        for s0, s1 in spans(GATHER_PLAN[0]):
            gather_words(0, s0, s1)
        quantise(1, 0, 128)
        quantise(1, 128, 384)
        quantise(1, 384, 512)
        for s0, s1 in spans(GATHER_PLAN[1]):
            gather_scales(s0, s1)
            for e in range(s0 // C, s1 // C):
                multiply(0, e)
            gather_words(1, s0, s1)
            for e in range(s0 // C, s1 // C):
                multiply(1, e)
                nc.scalar.activation(out=y[:, e * C:(e + 1) * C], in_=acc[e][:], func=silu, bias=b_sb[:, e:e + 1], scale=1.0)

        nc.vector.tensor_tensor(out=o1[:], in0=y[:].indirect(pos1_sb[:]), in1=gate_sb[:, 0, :], op=mult)
        for t0, t1 in spans(OUT_CHUNKS):
            nc.vector.tensor_tensor(out=o2[:, t0:t1], in0=y[:].indirect(pos2_sb[:, t0 // 16:t1 // 16]), in1=gate_sb[:, 1, t0:t1], op=mult)
        for t0, t1 in spans(OUT_CHUNKS):
            nc.vector.tensor_tensor(out=res[:, t0:t1], in0=o1[:, t0:t1], in1=o2[:, t0:t1], op=add)
            nc.sync.dma_start(out[:, t0:t1], res[:, t0:t1])
